import numpy as np
import ml_dtypes


def mxq(x, axis, fmt="e4m3"):
    dtype, down = {"e4m3": (ml_dtypes.float8_e4m3fn, 7), "e5m2": (ml_dtypes.float8_e5m2, 14)}[fmt]
    v = np.moveaxis(np.asarray(x, np.float32).astype(ml_dtypes.bfloat16).astype(np.float64), axis, -1)
    blocks = v.reshape(v.shape[:-1] + (-1, 32))
    amax = np.abs(blocks).max(-1, keepdims=True)
    byte = np.maximum(np.where(amax > 0, np.frexp(amax)[1] - 1 + 127, 0) - down, 1)
    scale = np.exp2(byte - 127.0)
    codes = (blocks / scale).astype(np.float32).astype(dtype).astype(np.float64)
    return np.moveaxis((codes * scale).reshape(v.shape), -1, axis)


WIDE = False


def mx_kscale(k):
    if not WIDE:
        return np.ones(k)
    levels = np.array([30, -30])
    if k % 512:
        return np.exp2(np.random.permutation(np.resize(levels, k // 32))).repeat(32)
    a = np.empty((k // 512, 16))
    for p in range(k // 512):
        a[p, :8] = np.random.permutation(np.resize(levels, 8))
        for g in range(8):
            far = levels[np.abs(levels - a[p, g]) >= 10]
            a[p, g + 8] = far[np.random.randint(len(far))]
    return np.exp2(a.ravel()).repeat(32)


def f64(x):
    return np.asarray(x).astype(np.float64)


def striped(idx):
    return np.tile(np.asarray(idx).reshape(-1, 16).T, (8, 1)).astype(np.uint16)


def unstriped(offs):
    return offs[:16].T.reshape(-1).astype(np.int64)


E2M1 = np.array([0.0, 0.5, 1.0, 1.5, 2.0, 3.0, 4.0, 6.0, -0.0, -0.5, -1.0, -1.5, -2.0, -3.0, -4.0, -6.0])


def pack_weight(w, fmt):
    k, n = w.shape
    w = f64(np.asarray(w, np.float32).astype(ml_dtypes.bfloat16)).reshape(k // 32, 32, n)
    amax = np.abs(w).max(1)
    if fmt == "e4m3":
        byte = np.frexp(amax)[1] - 1 + 127 - 7
    else:
        mant, ex = np.frexp(amax / 6.0)
        byte = np.where(mant > 0.5, ex, ex - 1) + 127
    byte = np.clip(np.where(amax > 0, byte, 1), 1, 254)
    scaled = (w * np.exp2(127.0 - byte)[:, None, :]).reshape(k, n).astype(np.float32)
    by_word = np.ascontiguousarray(scaled.reshape(k // 512, 128, 4, n).transpose(0, 1, 3, 2))
    if fmt == "e4m3":
        words = by_word.astype(ml_dtypes.float8_e4m3fn).view(np.uint8)
    else:
        c = by_word.astype(ml_dtypes.float4_e2m1fn).view(np.uint8) & 0xF
        words = (c[..., 0::2] | (c[..., 1::2] << 4)).reshape(k // 512, 128, 2 * n)
    return np.ascontiguousarray(words), np.ascontiguousarray(byte.astype(np.uint8).reshape(k // 512, 16, n))


def unpack_weight(words, scales, fmt):
    g, _, n = scales.shape
    words = np.ascontiguousarray(words).reshape(g, 128, n, -1)
    if fmt == "e4m3":
        vals = words.view(ml_dtypes.float8_e4m3fn).astype(np.float64)
    else:
        nib = np.empty((g, 128, n, 4), np.uint8)
        nib[..., 0::2] = words & 0xF
        nib[..., 1::2] = words >> 4
        vals = E2M1[nib]
    vals = vals * np.repeat(np.exp2(scales.astype(np.float64) - 127.0), 8, axis=1)[..., None]
    return vals.transpose(0, 1, 3, 2).reshape(g * 512, n)


N, K, T, J = 512, 512, 2048, 512


def setup_inputs():
    n = np.random.standard_normal
    idx = np.random.permutation(T)[:J]
    fn = mx_kscale(N)
    wp = pack_weight(n((N, K)) * 1 / np.sqrt(N) * fn[:, None], "e2m1")
    return {
        "g": (n((N, T))).astype(np.float32),
        "sv": (n((N, T))).astype(np.float32),
        "inv": (np.random.uniform(0.5, 2.0, (N, 1)) / fn[:, None]).astype(np.float32),
        "w_words": wp[0],
        "w_scales": wp[1],
        "res": (0.5 * n((K, J))).astype(np.float32),
        "offs": striped(idx),
    }


def reference(g, sv, inv, w_words, w_scales, res, offs):
    idx = unstriped(offs)
    wu = unpack_weight(w_words, w_scales, "e2m1")
    d = (f64(g)[:, idx] - f64(sv)[:, idx] * np.mean(f64(g)[:, idx] * f64(sv)[:, idx], axis=1, keepdims=True)) * f64(inv)
    dq = mxq(d, 0, "e5m2")
    p = wu.T @ dq
    y = p + f64(res)
    return y

@@ -1,0 +1,107 @@
+from contextlib import ExitStack
+
+import concourse.mybir as mybir
+
+N, K, T, J = 512, 512, 2048, 512
+FLOPS = 2 * N * K * J
+
+F32 = mybir.dt.float32
+BF16 = mybir.dt.bfloat16
+I32 = mybir.dt.int32
+U32 = mybir.dt.uint32
+U16 = mybir.dt.uint16
+U8 = mybir.dt.uint8
+E5M2X4 = mybir.dt.float8_e5m2_x4
+E2M1X4 = mybir.dt.float4_e2m1fn_x4
+MULT = mybir.AluOpType.mult
+ADD = mybir.AluOpType.add
+COPY = mybir.ActivationFunctionType.Copy
+
+P = 128
+PACK = 4
+M_TILE = 128
+SLOT_ORDER = (2, 0, 1, 3)
+SPLIT = 256
+
+
+def tile_list_evened_features_back_kernel(tc, g, sv, inv, w_words, w_scales, res, offs, out):
+    nc = tc.nc
+    with ExitStack() as ctx:
+        keep = ctx.enter_context(tc.tile_pool(name="keep", bufs=1))
+        psum = ctx.enter_context(tc.psum_pool(name="psum", bufs=1))
+
+        offsets = keep.tile([P, J // 16], U16, name="offsets")
+        inv_sb = keep.tile([P, PACK], F32, name="inv_sb")
+        w_codes = keep.tile([P, 2 * K], U8, name="w_codes", align_bytes=64)
+        w_scale = keep.tile([P, K], U8, name="w_scale", align_bytes=64)
+        res_sb = keep.tile([P, K // M_TILE, J], F32, name="res_sb")
+        d_grouped = keep.tile([P, J, PACK], BF16, name="d_grouped", align_bytes=64)
+        d_codes = keep.tile([P, J], U32, name="d_codes", align_bytes=64)
+        d_scale = keep.tile([P, J], U8, name="d_scale", align_bytes=64)
+
+        g_rows = g.rearrange("(p t) w -> p t w", t=PACK)
+        sv_rows = sv.rearrange("(p t) w -> p t w", t=PACK)
+        g_win = {}
+        sv_win = {}
+        for t in SLOT_ORDER:
+            g_win[t] = keep.tile([P, T], F32, name="g_win%d" % t)
+            sv_win[t] = keep.tile([P, T], F32, name="sv_win%d" % t)
+            nc.sync.dma_start(out=g_win[t][:], in_=g_rows[:, t, :])
+            if t == SLOT_ORDER[0]:
+                nc.sync.dma_start(offsets[:], offs)
+                nc.scalar.dma_start(out=inv_sb[:], in_=inv.rearrange("(p t) o -> p (t o)", t=PACK))
+            nc.sync.dma_start(out=sv_win[t][:], in_=sv_rows[:, t, :])
+
+        nc.gpsimd.memset(w_scale[:].bitcast(I32), 0)
+        nc.sync.dma_start(out=w_codes[:].bitcast(I32), in_=w_words[0].bitcast(I32))
+        for q in range(4):
+            nc.sync.dma_start(
+                out=w_scale[32 * q : 32 * q + 4, :].bitcast(I32),
+                in_=w_scales[0, 4 * q : 4 * q + 4, :].bitcast(I32),
+            )
+        nc.sync.dma_start(out=res_sb[:], in_=res.rearrange("(m p) j -> p m j", p=P))
+
+        for t in SLOT_ORDER:
+            g_pick = keep.tile([P, J], F32, name="g_pick%d" % t)
+            g_inv = keep.tile([P, J], F32, name="g_inv%d" % t)
+            sv_pick = keep.tile([P, J], F32, name="sv_pick%d" % t)
+            product = keep.tile([P, J], F32, name="product%d" % t)
+            coeff = keep.tile([P, 1], F32, name="coeff%d" % t)
+            d_flat = keep.tile([P, J], BF16, name="d_flat%d" % t)
+
+            nc.vector.tensor_copy(g_pick[:], g_win[t][:].indirect(offsets[:]))
+            nc.scalar.activation(g_inv[:], g_pick[:], COPY, scale=inv_sb[:, t : t + 1])
+            nc.vector.tensor_copy(sv_pick[:], sv_win[t][:].indirect(offsets[:]))
+            nc.vector.scalar_tensor_tensor(
+                product[:], sv_pick[:], -1.0 / J, g_inv[:], MULT, MULT, accum_out=coeff[:]
+            )
+            split = SPLIT if t >= 2 else J
+            nc.vector.scalar_tensor_tensor(
+                d_flat[:, 0:split], sv_pick[:, 0:split], coeff[:], g_inv[:, 0:split], MULT, ADD
+            )
+            nc.scalar.copy(d_grouped[:, 0:split, t], d_flat[:, 0:split])
+            if split < J:
+                nc.vector.scalar_tensor_tensor(
+                    d_grouped[:, split:J, t], sv_pick[:, split:J], coeff[:], g_inv[:, split:J], MULT, ADD
+                )
+
+        nc.vector.quantize_mx(
+            out=d_codes[:].bitcast(E5M2X4),
+            scales=d_scale[:],
+            in_=d_grouped[:].rearrange("p j t -> p (j t)"),
+        )
+
+        for m in range(K // M_TILE):
+            acc = psum.tile([M_TILE, J], F32, name="acc%d" % m)
+            nc.tensor.matmul_mx(
+                out=acc[:],
+                lhsT=w_codes[:, 2 * M_TILE * m : 2 * M_TILE * (m + 1)].bitcast(E2M1X4),
+                lhsT_scale=w_scale[:, M_TILE * m : M_TILE * (m + 1)],
+                rhs=d_codes[:].bitcast(E5M2X4),
+                rhs_scale=d_scale[:],
+                start=True,
+                stop=True,
+            )
+            result = keep.tile([M_TILE, J], F32, name="result%d" % m)
+            nc.vector.tensor_tensor(result[:], acc[:], res_sb[:, m, :], ADD)
+            nc.sync.dma_start(out=out[M_TILE * m : M_TILE * (m + 1), :], in_=result[:])

@@ -21,7 +21,9 @@ P = 128
 PACK = 4
 M_TILE = 128
 SLOT_ORDER = (2, 0, 1, 3)
-SPLIT = 256
+SCALAR_COLS = 192
+VECTOR_CUT = 352
+HALF = J // 2
 
 
 def tile_list_evened_features_back_kernel(tc, g, sv, inv, w_words, w_scales, res, offs, out):
@@ -75,21 +77,25 @@ def tile_list_evened_features_back_kernel(tc, g, sv, inv, w_words, w_scales, res
             nc.vector.scalar_tensor_tensor(
                 product[:], sv_pick[:], -1.0 / J, g_inv[:], MULT, MULT, accum_out=coeff[:]
             )
-            split = SPLIT if t >= 2 else J
-            nc.vector.scalar_tensor_tensor(
-                d_flat[:, 0:split], sv_pick[:, 0:split], coeff[:], g_inv[:, 0:split], MULT, ADD
-            )
-            nc.scalar.copy(d_grouped[:, 0:split, t], d_flat[:, 0:split])
-            if split < J:
+            if t < 2:
+                scalar_cols, vector_cols = slice(0, J), []
+            else:
+                scalar_cols = slice(0, SCALAR_COLS)
+                vector_cols = [slice(SCALAR_COLS, VECTOR_CUT), slice(VECTOR_CUT, J)]
+            for cols in [scalar_cols] + vector_cols:
                 nc.vector.scalar_tensor_tensor(
-                    d_grouped[:, split:J, t], sv_pick[:, split:J], coeff[:], g_inv[:, split:J], MULT, ADD
+                    d_flat[:, cols], sv_pick[:, cols], coeff[:], g_inv[:, cols], MULT, ADD
                 )
+            nc.scalar.copy(d_grouped[:, scalar_cols, t], d_flat[:, scalar_cols])
+            for cols in vector_cols:
+                nc.vector.tensor_copy(d_grouped[:, cols, t], d_flat[:, cols])
 
-        nc.vector.quantize_mx(
-            out=d_codes[:].bitcast(E5M2X4),
-            scales=d_scale[:],
-            in_=d_grouped[:].rearrange("p j t -> p (j t)"),
-        )
+        for cols in (slice(0, HALF), slice(HALF, J)):
+            nc.vector.quantize_mx(
+                out=d_codes[:, cols].bitcast(E5M2X4),
+                scales=d_scale[:, cols],
+                in_=d_grouped[:, cols, :].rearrange("p j t -> p (j t)"),
+            )
 
         for m in range(K // M_TILE):
             acc = psum.tile([M_TILE, J], F32, name="acc%d" % m)
@@ -103,5 +109,10 @@ def tile_list_evened_features_back_kernel(tc, g, sv, inv, w_words, w_scales, res
                 stop=True,
             )
             result = keep.tile([M_TILE, J], F32, name="result%d" % m)
-            nc.vector.tensor_tensor(result[:], acc[:], res_sb[:, m, :], ADD)
-            nc.sync.dma_start(out=out[M_TILE * m : M_TILE * (m + 1), :], in_=result[:])
+            if m in (0, K // M_TILE - 1):
+                pieces = [slice(0, HALF), slice(HALF, J)]
+            else:
+                pieces = [slice(0, J)]
+            for cols in pieces:
+                nc.vector.tensor_tensor(result[:, cols], acc[:, cols], res_sb[:, m, cols], ADD)
+                nc.sync.dma_start(out=out[M_TILE * m : M_TILE * (m + 1), cols], in_=result[:, cols])

@@ -65,17 +65,16 @@ def tile_list_evened_features_back_kernel(tc, g, sv, inv, w_words, w_scales, res
 
         for t in SLOT_ORDER:
             g_pick = keep.tile([P, J], F32, name="g_pick%d" % t)
-            g_inv = keep.tile([P, J], F32, name="g_inv%d" % t)
             sv_pick = keep.tile([P, J], F32, name="sv_pick%d" % t)
             product = keep.tile([P, J], F32, name="product%d" % t)
-            coeff = keep.tile([P, 1], F32, name="coeff%d" % t)
-            d_flat = keep.tile([P, J], BF16, name="d_flat%d" % t)
+            neg_mean = keep.tile([P, 1], F32, name="neg_mean%d" % t)
+            evened = keep.tile([P, J], F32, name="evened%d" % t)
+            factor = inv_sb[:, t : t + 1]
 
             nc.vector.tensor_copy(g_pick[:], g_win[t][:].indirect(offsets[:]))
-            nc.scalar.activation(g_inv[:], g_pick[:], COPY, scale=inv_sb[:, t : t + 1])
             nc.vector.tensor_copy(sv_pick[:], sv_win[t][:].indirect(offsets[:]))
             nc.vector.scalar_tensor_tensor(
-                product[:], sv_pick[:], -1.0 / J, g_inv[:], MULT, MULT, accum_out=coeff[:]
+                product[:], sv_pick[:], -1.0 / J, g_pick[:], MULT, MULT, accum_out=neg_mean[:]
             )
             if t < 2:
                 scalar_cols, vector_cols = slice(0, J), []
@@ -84,11 +83,11 @@ def tile_list_evened_features_back_kernel(tc, g, sv, inv, w_words, w_scales, res
                 vector_cols = [slice(SCALAR_COLS, VECTOR_CUT), slice(VECTOR_CUT, J)]
             for cols in [scalar_cols] + vector_cols:
                 nc.vector.scalar_tensor_tensor(
-                    d_flat[:, cols], sv_pick[:, cols], coeff[:], g_inv[:, cols], MULT, ADD
+                    evened[:, cols], sv_pick[:, cols], neg_mean[:], g_pick[:, cols], MULT, ADD
                 )
-            nc.scalar.copy(d_grouped[:, scalar_cols, t], d_flat[:, scalar_cols])
+            nc.scalar.activation(d_grouped[:, scalar_cols, t], evened[:, scalar_cols], COPY, scale=factor)
             for cols in vector_cols:
-                nc.vector.tensor_copy(d_grouped[:, cols, t], d_flat[:, cols])
+                nc.vector.tensor_scalar(d_grouped[:, cols, t], evened[:, cols], factor, None, MULT)
 
         for cols in (slice(0, HALF), slice(HALF, J)):
             nc.vector.quantize_mx(
@@ -109,10 +108,5 @@ def tile_list_evened_features_back_kernel(tc, g, sv, inv, w_words, w_scales, res
                 stop=True,
             )
             result = keep.tile([M_TILE, J], F32, name="result%d" % m)
-            if m in (0, K // M_TILE - 1):
-                pieces = [slice(0, HALF), slice(HALF, J)]
-            else:
-                pieces = [slice(0, J)]
-            for cols in pieces:
-                nc.vector.tensor_tensor(result[:, cols], acc[:, cols], res_sb[:, m, cols], ADD)
-                nc.sync.dma_start(out=out[M_TILE * m : M_TILE * (m + 1), cols], in_=result[:, cols])
+            nc.vector.tensor_tensor(result[:], acc[:], res_sb[:, m, :], ADD)
+            nc.sync.dma_start(out=out[M_TILE * m : M_TILE * (m + 1), :], in_=result[:])

from contextlib import ExitStack

import concourse.mybir as mybir

N, K, T, J = 512, 512, 2048, 512
FLOPS = 2 * N * K * J

F32 = mybir.dt.float32
BF16 = mybir.dt.bfloat16
I32 = mybir.dt.int32
U32 = mybir.dt.uint32
U16 = mybir.dt.uint16
U8 = mybir.dt.uint8
E5M2X4 = mybir.dt.float8_e5m2_x4
E2M1X4 = mybir.dt.float4_e2m1fn_x4
MULT = mybir.AluOpType.mult
ADD = mybir.AluOpType.add
COPY = mybir.ActivationFunctionType.Copy

P = 128
PACK = 4
M_TILE = 128
SLOT_ORDER = (2, 0, 1, 3)
SCALAR_COLS = 192
VECTOR_CUT = 352
HALF = J // 2


def tile_list_evened_features_back_kernel(tc, g, sv, inv, w_words, w_scales, res, offs, out):
    nc = tc.nc
    with ExitStack() as ctx:
        keep = ctx.enter_context(tc.tile_pool(name="keep", bufs=1))
        psum = ctx.enter_context(tc.psum_pool(name="psum", bufs=1))

        offsets = keep.tile([P, J // 16], U16, name="offsets")
        inv_sb = keep.tile([P, PACK], F32, name="inv_sb")
        w_codes = keep.tile([P, 2 * K], U8, name="w_codes", align_bytes=64)
        w_scale = keep.tile([P, K], U8, name="w_scale", align_bytes=64)
        res_sb = keep.tile([P, K // M_TILE, J], F32, name="res_sb")
        d_grouped = keep.tile([P, J, PACK], BF16, name="d_grouped", align_bytes=64)
        d_codes = keep.tile([P, J], U32, name="d_codes", align_bytes=64)
        d_scale = keep.tile([P, J], U8, name="d_scale", align_bytes=64)

        g_rows = g.rearrange("(p t) w -> p t w", t=PACK)
        sv_rows = sv.rearrange("(p t) w -> p t w", t=PACK)
        g_win = {}
        sv_win = {}
        for t in SLOT_ORDER:
            g_win[t] = keep.tile([P, T], F32, name="g_win%d" % t)
            sv_win[t] = keep.tile([P, T], F32, name="sv_win%d" % t)
            nc.sync.dma_start(out=g_win[t][:], in_=g_rows[:, t, :])
            if t == SLOT_ORDER[0]:
                nc.sync.dma_start(offsets[:], offs)
                nc.scalar.dma_start(out=inv_sb[:], in_=inv.rearrange("(p t) o -> p (t o)", t=PACK))
            nc.sync.dma_start(out=sv_win[t][:], in_=sv_rows[:, t, :])

        nc.gpsimd.memset(w_scale[:].bitcast(I32), 0)
        nc.sync.dma_start(out=w_codes[:].bitcast(I32), in_=w_words[0].bitcast(I32))
        for q in range(4):
            nc.sync.dma_start(
                out=w_scale[32 * q : 32 * q + 4, :].bitcast(I32),
                in_=w_scales[0, 4 * q : 4 * q + 4, :].bitcast(I32),
            )
        nc.sync.dma_start(out=res_sb[:], in_=res.rearrange("(m p) j -> p m j", p=P))

        for t in SLOT_ORDER:
            g_pick = keep.tile([P, J], F32, name="g_pick%d" % t)
            sv_pick = keep.tile([P, J], F32, name="sv_pick%d" % t)
            product = keep.tile([P, J], F32, name="product%d" % t)
            neg_mean = keep.tile([P, 1], F32, name="neg_mean%d" % t)
            evened = keep.tile([P, J], F32, name="evened%d" % t)
            factor = inv_sb[:, t : t + 1]

            nc.vector.tensor_copy(g_pick[:], g_win[t][:].indirect(offsets[:]))
            nc.vector.tensor_copy(sv_pick[:], sv_win[t][:].indirect(offsets[:]))
            nc.vector.scalar_tensor_tensor(
                product[:], sv_pick[:], -1.0 / J, g_pick[:], MULT, MULT, accum_out=neg_mean[:]
            )
            if t < 2:
                scalar_cols, vector_cols = slice(0, J), []
            else:
                scalar_cols = slice(0, SCALAR_COLS)
                vector_cols = [slice(SCALAR_COLS, VECTOR_CUT), slice(VECTOR_CUT, J)]
            for cols in [scalar_cols] + vector_cols:
                nc.vector.scalar_tensor_tensor(
                    evened[:, cols], sv_pick[:, cols], neg_mean[:], g_pick[:, cols], MULT, ADD
                )
            nc.scalar.activation(d_grouped[:, scalar_cols, t], evened[:, scalar_cols], COPY, scale=factor)
            for cols in vector_cols:
                nc.vector.tensor_scalar(d_grouped[:, cols, t], evened[:, cols], factor, None, MULT)

        for cols in (slice(0, HALF), slice(HALF, J)):
            nc.vector.quantize_mx(
                out=d_codes[:, cols].bitcast(E5M2X4),
                scales=d_scale[:, cols],
                in_=d_grouped[:, cols, :].rearrange("p j t -> p (j t)"),
            )

        for m in range(K // M_TILE):
            acc = psum.tile([M_TILE, J], F32, name="acc%d" % m)
            nc.tensor.matmul_mx(
                out=acc[:],
                lhsT=w_codes[:, 2 * M_TILE * m : 2 * M_TILE * (m + 1)].bitcast(E2M1X4),
                lhsT_scale=w_scale[:, M_TILE * m : M_TILE * (m + 1)],
                rhs=d_codes[:].bitcast(E5M2X4),
                rhs_scale=d_scale[:],
                start=True,
                stop=True,
            )
            result = keep.tile([M_TILE, J], F32, name="result%d" % m)
            nc.vector.tensor_tensor(result[:], acc[:], res_sb[:, m, :], ADD)
            nc.sync.dma_start(out=out[M_TILE * m : M_TILE * (m + 1), :], in_=result[:])
